import numpy as np
import ml_dtypes


def mxq(x, axis, fmt="e4m3"):
    dtype, down = {"e4m3": (ml_dtypes.float8_e4m3fn, 7), "e5m2": (ml_dtypes.float8_e5m2, 14)}[fmt]
    v = np.moveaxis(np.asarray(x, np.float32).astype(ml_dtypes.bfloat16).astype(np.float64), axis, -1)
    blocks = v.reshape(v.shape[:-1] + (-1, 32))
    amax = np.abs(blocks).max(-1, keepdims=True)
    byte = np.maximum(np.where(amax > 0, np.frexp(amax)[1] - 1 + 127, 0) - down, 1)
    scale = np.exp2(byte - 127.0)
    codes = (blocks / scale).astype(np.float32).astype(dtype).astype(np.float64)
    return np.moveaxis((codes * scale).reshape(v.shape), -1, axis)


WIDE = False


def mx_kscale(k):
    if not WIDE:
        return np.ones(k)
    levels = np.array([10, -10, 5, -5, 0])
    if k % 512:
        return np.exp2(np.random.permutation(np.resize(levels, k // 32))).repeat(32)
    a = np.empty((k // 512, 16))
    for p in range(k // 512):
        a[p, :8] = np.random.permutation(np.resize(levels, 8))
        for g in range(8):
            far = levels[np.abs(levels - a[p, g]) >= 10]
            a[p, g + 8] = far[np.random.randint(len(far))]
    return np.exp2(a.ravel()).repeat(32)


def f64(x):
    return np.asarray(x).astype(np.float64)


def striped(idx):
    return np.tile(idx.reshape(-1, 16).T, (8, 1)).astype(np.uint16)


def unstriped(offs):
    return offs[:16].T.reshape(-1).astype(np.int64)


def pack_weight(w):
    k, n = w.shape
    w = f64(np.asarray(w, np.float32).astype(ml_dtypes.bfloat16)).reshape(k // 32, 32, n)
    amax = np.abs(w).max(1)
    byte = np.clip(np.where(amax > 0, np.frexp(amax)[1] - 1 + 127 - 7, 1), 1, 254)
    scaled = (w * np.exp2(127.0 - byte)[:, None, :]).reshape(k, n).astype(np.float32)
    words = np.ascontiguousarray(scaled.reshape(k // 512, 128, 4, n).transpose(0, 1, 3, 2)).astype(ml_dtypes.float8_e4m3fn).view(np.uint8)
    return words, np.ascontiguousarray(byte.astype(np.uint8).reshape(k // 512, 16, n))


def unpack_weight(words, scales):
    g, p, n, _ = words.shape
    vals = np.ascontiguousarray(words).view(ml_dtypes.float8_e4m3fn).astype(np.float64) * np.repeat(np.exp2(scales.astype(np.float64) - 127.0), 8, axis=1)[..., None]
    return vals.transpose(0, 1, 3, 2).reshape(g * 512, n)


K, T, S, N, U = 1024, 2048, 512, 128, 1024


def setup_inputs():
    n = np.random.standard_normal
    s = mx_kscale(K)[:, None]
    packed_xT = pack_weight(n((K, T)) * s)
    return {
        "x_words": packed_xT[0],
        "x_scales": packed_xT[1],
        "w1": (n((K, N)) / np.sqrt(K) / s).astype(np.float32),
        "vs": (np.random.uniform(0.1, 2.0, (N, U))).astype(np.float32),
        "ws": (n((N, U))).astype(np.float32),
        "rate": (np.random.uniform(0.3, 1.2, (N, 1))).astype(np.float32),
        "offs": striped(np.random.permutation(T)[:S]),
        "slot": striped(np.random.permutation(U)[:S]),
    }


def reference(x_words, x_scales, w1, vs, ws, rate, offs, slot):
    xq = unpack_weight(x_words, x_scales)[:, unstriped(offs)]
    y = mxq(f64(w1), 0, "e4m3").T @ xq
    vsg = f64(vs)[:, unstriped(slot)]
    vnew = 0.8 * vsg + 0.2 * ((y) ** 2)
    wsg = f64(ws)[:, unstriped(slot)]
    upd = y / (np.sqrt(vnew) + 0.1) + 0.1 * wsg
    wsq = (wsg) ** 2
    wnorm = np.sqrt(wsq.mean(axis=1, keepdims=True) + 0.01)
    u2 = (upd) ** 2
    unorm = np.sqrt(u2.mean(axis=1, keepdims=True) + 0.01)
    stp = (upd * wnorm) / unorm
    return (f64(rate) * np.tanh(stp)) * np.sqrt(vnew)

@@ -1,0 +1,159 @@
+from contextlib import ExitStack
+
+import concourse.mybir as mybir
+
+K, T, S, N, U = 1024, 2048, 512, 128, 1024
+FLOPS = 2 * K * N * S
+
+F32 = mybir.dt.float32
+BF16 = mybir.dt.bfloat16
+I32 = mybir.dt.int32
+U32 = mybir.dt.uint32
+U16 = mybir.dt.uint16
+U8 = mybir.dt.uint8
+FP8X4 = mybir.dt.float8_e4m3fn_x4
+ACT = mybir.ActivationFunctionType
+ALU = mybir.AluOpType
+
+P = 128
+PACK = 4
+PASSES = K // (P * PACK)
+HALVES = 2
+H = S // HALVES
+MM = 4
+MW = S // MM
+CH = 4
+CW = S // CH
+FCH = 4
+FW = S // FCH
+
+
+def tile_picked_ylamb_bnd_p_kernel(
+    tc, x_words, x_scales, w1, vs, ws, rate, offs, slot, out
+):
+    nc = tc.nc
+    with ExitStack() as ctx:
+        pool = ctx.enter_context(tc.tile_pool(name="held", bufs=1))
+        psum = ctx.enter_context(tc.psum_pool(name="psum", bufs=1))
+
+        slot_sb = pool.tile([P, S // 16], U16, name="slot_sb")
+        offs_sb = pool.tile([P, S // 16], U16, name="offs_sb")
+        ws_sb = pool.tile([P, U], F32, name="ws_sb")
+        vs_sb = pool.tile([P, U], F32, name="vs_sb")
+        w_raw = pool.tile([P, PASSES, PACK, N], F32, name="w_raw")
+        x_sb = [pool.tile([P, T], I32, name="x_sb%d" % o) for o in range(PASSES)]
+        xs_sb = pool.tile([P, T], U8, name="xs_sb")
+        rate_sb = pool.tile([P, 1], F32, name="rate_sb")
+        ones = pool.tile([P, 1], F32, name="ones")
+        minus_half = pool.tile([P, 1], F32, name="minus_half")
+        upd = pool.tile([P, S + 1], F32, name="upd")
+
+        nc.vector.memset(ones[:], 1.0)
+        nc.gpsimd.memset(xs_sb[:].bitcast(I32), 0)
+        nc.gpsimd.memset(minus_half[:], -0.5)
+        nc.scalar.activation(upd[:, S : S + 1], ones[:], ACT.Abs_reciprocal_sqrt, scale=1.0 / (0.01 * S))
+
+        def load_scales(engine):
+            for q in range(4):
+                engine.dma_start(
+                    xs_sb[32 * q : 32 * q + 4 * PASSES, :].bitcast(I32),
+                    x_scales[:, 4 * q : 4 * q + 4, :].bitcast(I32),
+                )
+
+        def load_w():
+            nc.sync.dma_start(
+                w_raw[:].rearrange("p o j n -> p o (j n)"),
+                w1.rearrange("(o p j) n -> p o (j n)", o=PASSES, j=PACK),
+            )
+
+        def load_x(o):
+            nc.sync.dma_start(x_sb[o][:], x_words[o].rearrange("p c r -> p (c r)").bitcast(I32))
+
+        nc.sync.dma_start(slot_sb[:], slot)
+        nc.sync.dma_start(offs_sb[:], offs)
+        nc.sync.dma_start(ws_sb[:], ws)
+        load_scales(nc.sync)
+        load_w()
+        load_x(0)
+        load_x(1)
+        nc.sync.dma_start(vs_sb[:], vs)
+        nc.sync.dma_start(rate_sb[:], rate)
+
+        wsg = pool.tile([P, S], F32, name="wsg")
+        nc.vector.tensor_copy(wsg[:], ws_sb[:].indirect(slot_sb[:]))
+
+        xg_scales = pool.tile([P, S], U8, name="xg_scales", align_bytes=64)
+        nc.vector.tensor_copy(xg_scales[:], xs_sb[:].indirect(offs_sb[:]))
+
+        w_bf = pool.tile([P, PASSES, N, PACK], BF16, name="w_bf", align_bytes=64)
+        nc.scalar.copy(w_bf[:], w_raw[:].rearrange("p o j n -> p o n j"))
+        w_codes = pool.tile([P, PASSES * N], U32, name="w_codes", align_bytes=64)
+        w_scales = pool.tile([P, PASSES * N], U8, name="w_scales", align_bytes=64)
+        nc.vector.quantize_mx(
+            out=w_codes[:].bitcast(FP8X4), scales=w_scales[:], in_=w_bf[:].rearrange("p o n j -> p (o n j)")
+        )
+        junk_w = pool.tile([P, S], F32, name="junk_w")
+        wsum = pool.tile([P, 1], F32, name="wsum")
+        nc.scalar.activation(junk_w[:], wsg[:], ACT.Square, accum_out=wsum[:])
+        wden = pool.tile([P, 1], F32, name="wden")
+        nc.vector.tensor_scalar(wden[:], wsum[:], 0.01 * S, None, ALU.add)
+        winv = pool.tile([P, 1], F32, name="winv")
+        nc.vector.reciprocal(winv[:], wden[:])
+
+        y = [psum.tile([P, MW], F32, name="y%d" % m) for m in range(MM)]
+        for o in range(PASSES):
+            for h in range(HALVES):
+                xg = pool.tile([P, H], U32, name="xg%d_%d" % (o, h), align_bytes=64)
+                nc.vector.tensor_copy(
+                    xg[:], x_sb[o][:].bitcast(U32).indirect(offs_sb[:, h * H // 16 : (h + 1) * H // 16])
+                )
+                for m in range(h * MM // HALVES, (h + 1) * MM // HALVES):
+                    nc.tensor.matmul_mx(
+                        out=y[m][:],
+                        lhsT=w_codes[:, o * N : (o + 1) * N].bitcast(FP8X4),
+                        lhsT_scale=w_scales[:, o * N : (o + 1) * N],
+                        rhs=xg[:, m * MW - h * H : (m + 1) * MW - h * H].bitcast(FP8X4),
+                        rhs_scale=xg_scales[4 * o :, m * MW : (m + 1) * MW],
+                        start=(o == 0),
+                        stop=(o == PASSES - 1),
+                    )
+
+        def y_cols(c):
+            m = c * CW // MW
+            return y[m][:, c * CW - m * MW : (c + 1) * CW - m * MW]
+
+        sq, t, a, e, r, q_t, g, th, res = [
+            pool.tile([P, S], F32, name=n) for n in ("sq", "t", "a", "e", "r", "q", "g", "th", "res")
+        ]
+        chunks = [slice(c * CW, (c + 1) * CW) for c in range(CH)]
+        for c, cols in enumerate(chunks):
+            nc.scalar.activation(sq[:, cols], y_cols(c), ACT.Square, scale=0.5)
+        for c, cols in enumerate(chunks):
+            nc.vector.tensor_tensor(
+                t[:, cols], vs_sb[:].indirect(slot_sb[:, c * CW // 16 : (c + 1) * CW // 16]), sq[:, cols], ALU.add
+            )
+        for cols in chunks:
+            nc.scalar.activation(a[:, cols], t[:, cols], ACT.Abs_reciprocal_sqrt, scale=0.8, bias=1e-30)
+        for cols in chunks:
+            nc.vector.scalar_tensor_tensor(e[:, cols], a[:, cols], 5.0, t[:, cols], ALU.add, ALU.mult)
+        for cols in chunks:
+            nc.scalar.activation(r[:, cols], e[:, cols], ACT.Abs_reciprocal_sqrt, scale=0.16, bias=0.01)
+        for c, cols in enumerate(chunks):
+            nc.vector.tensor_tensor(q_t[:, cols], y_cols(c), r[:, cols], ALU.mult)
+        for cols in chunks:
+            nc.vector.scalar_tensor_tensor(upd[:, cols], wsg[:, cols], 0.1, q_t[:, cols], ALU.mult, ALU.add)
+        junk_u = pool.tile([P, S + 1], F32, name="junk_u")
+        quot = pool.tile([P, 1], F32, name="quot")
+        nc.vector.scalar_tensor_tensor(junk_u[:], upd[:], winv[:], upd[:], ALU.mult, ALU.mult, accum_out=quot[:])
+        ratio = pool.tile([P, 1], F32, name="ratio")
+        nc.gpsimd.tensor_tensor(ratio[:], quot[:], minus_half[:], ALU.pow)
+        rate08 = pool.tile([P, 1], F32, name="rate08")
+        nc.vector.tensor_scalar(rate08[:], rate_sb[:], 0.8, None, ALU.mult)
+        g = junk_u
+        fchunks = [slice(c * FW, (c + 1) * FW) for c in range(FCH)]
+        for cols in chunks:
+            nc.vector.scalar_tensor_tensor(g[:, cols], t[:, cols], rate08[:], a[:, cols], ALU.mult, ALU.mult)
+        for cols in fchunks:
+            nc.scalar.activation(th[:, cols], upd[:, cols], ACT.Tanh, scale=ratio[:])
+            nc.vector.tensor_tensor(res[:, cols], th[:, cols], g[:, cols], ALU.mult)
+            nc.sync.dma_start(out[:, cols], res[:, cols])

@@ -54,11 +54,8 @@ def tile_picked_ylamb_bnd_p_kernel(
         nc.scalar.activation(upd[:, S : S + 1], ones[:], ACT.Abs_reciprocal_sqrt, scale=1.0 / (0.01 * S))
 
         def load_scales(engine):
-            for q in range(4):
-                engine.dma_start(
-                    xs_sb[32 * q : 32 * q + 4 * PASSES, :].bitcast(I32),
-                    x_scales[:, 4 * q : 4 * q + 4, :].bitcast(I32),
-                )
+            for o in range(PASSES):
+                engine.dma_start(xs_sb[4 * o : P : 8, :].bitcast(I32), x_scales[o].bitcast(I32))
 
         def load_w():
             nc.sync.dma_start(
@@ -69,24 +66,32 @@ def tile_picked_ylamb_bnd_p_kernel(
         def load_x(o):
             nc.sync.dma_start(x_sb[o][:], x_words[o].rearrange("p c r -> p (c r)").bitcast(I32))
 
-        nc.sync.dma_start(slot_sb[:], slot)
         nc.sync.dma_start(offs_sb[:], offs)
-        nc.sync.dma_start(ws_sb[:], ws)
         load_scales(nc.sync)
+        nc.sync.dma_start(slot_sb[:], slot)
+        nc.sync.dma_start(ws_sb[:], ws)
         load_w()
         load_x(0)
         load_x(1)
         nc.sync.dma_start(vs_sb[:], vs)
         nc.sync.dma_start(rate_sb[:], rate)
 
+        xg_spread = pool.tile([P, S], U8, name="xg_spread", align_bytes=64)
+        nc.vector.tensor_copy(xg_spread[:], xs_sb[:].indirect(offs_sb[:]))
+        xg_scales = pool.tile([P, S], U8, name="xg_scales", align_bytes=64)
+        for row in range(4):
+            count = 32 if row == 0 else 26
+            nc.scalar.dma_start(
+                xg_scales[row : row + 4 * (count - 1) + 1 : 4, :].bitcast(I32),
+                xg_spread[8 * row : 8 * row + 4 * (count - 1) + 1 : 4, :].bitcast(I32),
+            )
+
         wsg = pool.tile([P, S], F32, name="wsg")
         nc.vector.tensor_copy(wsg[:], ws_sb[:].indirect(slot_sb[:]))
 
-        xg_scales = pool.tile([P, S], U8, name="xg_scales", align_bytes=64)
-        nc.vector.tensor_copy(xg_scales[:], xs_sb[:].indirect(offs_sb[:]))
 
         w_bf = pool.tile([P, PASSES, N, PACK], BF16, name="w_bf", align_bytes=64)
-        nc.scalar.copy(w_bf[:], w_raw[:].rearrange("p o j n -> p o n j"))
+        nc.vector.tensor_copy(w_bf[:], w_raw[:].rearrange("p o j n -> p o n j"))
         w_codes = pool.tile([P, PASSES * N], U32, name="w_codes", align_bytes=64)
         w_scales = pool.tile([P, PASSES * N], U8, name="w_scales", align_bytes=64)
         nc.vector.quantize_mx(
@@ -128,10 +133,11 @@ def tile_picked_ylamb_bnd_p_kernel(
         chunks = [slice(c * CW, (c + 1) * CW) for c in range(CH)]
         for c, cols in enumerate(chunks):
             nc.scalar.activation(sq[:, cols], y_cols(c), ACT.Square, scale=0.5)
+        vsg0 = pool.tile([P, CW], F32, name="vsg0")
+        nc.vector.tensor_copy(vsg0[:], vs_sb[:].indirect(slot_sb[:, 0 : CW // 16]))
         for c, cols in enumerate(chunks):
-            nc.vector.tensor_tensor(
-                t[:, cols], vs_sb[:].indirect(slot_sb[:, c * CW // 16 : (c + 1) * CW // 16]), sq[:, cols], ALU.add
-            )
+            looked_up = vsg0[:] if c == 0 else vs_sb[:].indirect(slot_sb[:, c * CW // 16 : (c + 1) * CW // 16])
+            nc.vector.tensor_tensor(t[:, cols], looked_up, sq[:, cols], ALU.add)
         for cols in chunks:
             nc.scalar.activation(a[:, cols], t[:, cols], ACT.Abs_reciprocal_sqrt, scale=0.8, bias=1e-30)
         for cols in chunks:

@@ -18,148 +18,155 @@ ALU = mybir.AluOpType
 P = 128
 PACK = 4
 PASSES = K // (P * PACK)
-HALVES = 2
-H = S // HALVES
-MM = 4
-MW = S // MM
-CH = 4
-CW = S // CH
-FCH = 4
-FW = S // FCH
+QUADRANT = 32
+ROWS = 4
+BLOCK_PARTS = 8
+LIST_COL = 16
+HALF = S // 2
+CHUNKS = 4
+CHUNK = S // CHUNKS
+NORM_EPS = 0.01 * S
+TINY = 1e-30
 
 
 def tile_picked_ylamb_bnd_p_kernel(
     tc, x_words, x_scales, w1, vs, ws, rate, offs, slot, out
 ):
     nc = tc.nc
+    halves = [slice(h * HALF, (h + 1) * HALF) for h in range(2)]
+    chunks = [slice(c * CHUNK, (c + 1) * CHUNK) for c in range(CHUNKS)]
+
+    def entries(list_tile, cols):
+        return list_tile[:, cols.start // LIST_COL : cols.stop // LIST_COL]
+
     with ExitStack() as ctx:
         pool = ctx.enter_context(tc.tile_pool(name="held", bufs=1))
         psum = ctx.enter_context(tc.psum_pool(name="psum", bufs=1))
 
-        slot_sb = pool.tile([P, S // 16], U16, name="slot_sb")
-        offs_sb = pool.tile([P, S // 16], U16, name="offs_sb")
+        slot_sb = pool.tile([P, S // LIST_COL], U16, name="slot_sb")
+        offs_sb = pool.tile([P, S // LIST_COL], U16, name="offs_sb")
         ws_sb = pool.tile([P, U], F32, name="ws_sb")
-        vs_sb = pool.tile([P, U], F32, name="vs_sb")
-        w_raw = pool.tile([P, PASSES, PACK, N], F32, name="w_raw")
+        w_raw = [pool.tile([P, PACK, N], F32, name="w_raw%d" % o) for o in range(PASSES)]
         x_sb = [pool.tile([P, T], I32, name="x_sb%d" % o) for o in range(PASSES)]
         xs_sb = pool.tile([P, T], U8, name="xs_sb")
-        rate_sb = pool.tile([P, 1], F32, name="rate_sb")
         ones = pool.tile([P, 1], F32, name="ones")
         minus_half = pool.tile([P, 1], F32, name="minus_half")
         upd = pool.tile([P, S + 1], F32, name="upd")
 
+        nc.vector.memset(xs_sb[:].bitcast(I32), 0)
         nc.vector.memset(ones[:], 1.0)
-        nc.gpsimd.memset(xs_sb[:].bitcast(I32), 0)
         nc.gpsimd.memset(minus_half[:], -0.5)
-        nc.scalar.activation(upd[:, S : S + 1], ones[:], ACT.Abs_reciprocal_sqrt, scale=1.0 / (0.01 * S))
+        nc.scalar.activation(upd[:, S : S + 1], ones[:], ACT.Abs_reciprocal_sqrt, scale=1.0 / NORM_EPS)
 
-        def load_scales(engine):
-            for o in range(PASSES):
-                engine.dma_start(xs_sb[4 * o : P : 8, :].bitcast(I32), x_scales[o].bitcast(I32))
-
-        def load_w():
-            nc.sync.dma_start(
-                w_raw[:].rearrange("p o j n -> p o (j n)"),
-                w1.rearrange("(o p j) n -> p o (j n)", o=PASSES, j=PACK),
-            )
-
-        def load_x(o):
-            nc.sync.dma_start(x_sb[o][:], x_words[o].rearrange("p c r -> p (c r)").bitcast(I32))
+        def load_w(o):
+            rows = w1[o * P * PACK : (o + 1) * P * PACK, :]
+            nc.sync.dma_start(w_raw[o][:].rearrange("p j n -> p (j n)"), rows.rearrange("(p j) n -> p (j n)", j=PACK))
 
         nc.sync.dma_start(offs_sb[:], offs)
-        load_scales(nc.sync)
         nc.sync.dma_start(slot_sb[:], slot)
+        load_w(0)
+        for o in range(PASSES):
+            nc.sync.dma_start(xs_sb[ROWS * o : P : BLOCK_PARTS, :].bitcast(I32), x_scales[o].bitcast(I32))
         nc.sync.dma_start(ws_sb[:], ws)
-        load_w()
-        load_x(0)
-        load_x(1)
-        nc.sync.dma_start(vs_sb[:], vs)
-        nc.sync.dma_start(rate_sb[:], rate)
+        load_w(1)
+        for o in range(PASSES):
+            nc.sync.dma_start(x_sb[o][:], x_words[o].rearrange("p c r -> p (c r)").bitcast(I32))
 
         xg_spread = pool.tile([P, S], U8, name="xg_spread", align_bytes=64)
         nc.vector.tensor_copy(xg_spread[:], xs_sb[:].indirect(offs_sb[:]))
         xg_scales = pool.tile([P, S], U8, name="xg_scales", align_bytes=64)
-        for row in range(4):
-            count = 32 if row == 0 else 26
-            nc.scalar.dma_start(
-                xg_scales[row : row + 4 * (count - 1) + 1 : 4, :].bitcast(I32),
-                xg_spread[8 * row : 8 * row + 4 * (count - 1) + 1 : 4, :].bitcast(I32),
-            )
+        nc.vector.tensor_copy(xg_scales[:].bitcast(I32), xg_spread[:].bitcast(I32))
+        for o in range(PASSES):
+            for i in range(1, ROWS):
+                nc.sync.dma_start(
+                    xg_scales[ROWS * o + i : P : QUADRANT, :].bitcast(I32),
+                    xg_spread[ROWS * o + BLOCK_PARTS * i : P : QUADRANT, :].bitcast(I32),
+                )
 
         wsg = pool.tile([P, S], F32, name="wsg")
         nc.vector.tensor_copy(wsg[:], ws_sb[:].indirect(slot_sb[:]))
 
-
-        w_bf = pool.tile([P, PASSES, N, PACK], BF16, name="w_bf", align_bytes=64)
-        nc.vector.tensor_copy(w_bf[:], w_raw[:].rearrange("p o j n -> p o n j"))
+        w_bf = pool.tile([P, PASSES, N, PACK], BF16, name="w_bf", tag="w_then_vs", align_bytes=64)
+        for o in range(PASSES):
+            nc.scalar.copy(w_bf[:, o], w_raw[o][:].rearrange("p j n -> p n j"))
         w_codes = pool.tile([P, PASSES * N], U32, name="w_codes", align_bytes=64)
         w_scales = pool.tile([P, PASSES * N], U8, name="w_scales", align_bytes=64)
         nc.vector.quantize_mx(
             out=w_codes[:].bitcast(FP8X4), scales=w_scales[:], in_=w_bf[:].rearrange("p o n j -> p (o n j)")
         )
-        junk_w = pool.tile([P, S], F32, name="junk_w")
-        wsum = pool.tile([P, 1], F32, name="wsum")
-        nc.scalar.activation(junk_w[:], wsg[:], ACT.Square, accum_out=wsum[:])
-        wden = pool.tile([P, 1], F32, name="wden")
-        nc.vector.tensor_scalar(wden[:], wsum[:], 0.01 * S, None, ALU.add)
-        winv = pool.tile([P, 1], F32, name="winv")
-        nc.vector.reciprocal(winv[:], wden[:])
 
-        y = [psum.tile([P, MW], F32, name="y%d" % m) for m in range(MM)]
-        for o in range(PASSES):
-            for h in range(HALVES):
-                xg = pool.tile([P, H], U32, name="xg%d_%d" % (o, h), align_bytes=64)
-                nc.vector.tensor_copy(
-                    xg[:], x_sb[o][:].bitcast(U32).indirect(offs_sb[:, h * H // 16 : (h + 1) * H // 16])
-                )
-                for m in range(h * MM // HALVES, (h + 1) * MM // HALVES):
+        vs_sb = pool.tile([P, U], F32, name="vs_sb", tag="w_then_vs", align_bytes=64)
+        nc.sync.dma_start(vs_sb[:], vs)
+
+        wsq = pool.tile([P, S], F32, name="wsq")
+        wsq_sum = pool.tile([P, 1], F32, name="wsq_sum")
+        nc.scalar.activation(wsq[:], wsg[:], ACT.Square, accum_out=wsq_sum[:])
+
+        def gather_words(o):
+            tiles = [pool.tile([P, HALF], U32, name="xg%d_%d" % (o, h), align_bytes=64) for h in range(2)]
+            for tile, cols in zip(tiles, halves):
+                nc.vector.tensor_copy(tile[:], x_sb[o][:].bitcast(U32).indirect(entries(offs_sb, cols)))
+            return tiles
+
+        xg = [gather_words(0)]
+        w_den = pool.tile([P, 1], F32, name="w_den", tag="w_den_then_rate")
+        nc.vector.tensor_scalar(w_den[:], wsq_sum[:], NORM_EPS, None, ALU.add)
+        w_inv = pool.tile([P, 1], F32, name="w_inv")
+        nc.vector.reciprocal(w_inv[:], w_den[:])
+        rate_sb = pool.tile([P, 1], F32, name="rate_sb", tag="w_den_then_rate")
+        nc.sync.dma_start(rate_sb[:], rate)
+        xg.append(gather_words(1))
+
+        y = [psum.tile([P, CHUNK], F32, name="y%d" % c) for c in range(CHUNKS)]
+        for h, half in enumerate(halves):
+            for o in range(PASSES):
+                for c in range(half.start // CHUNK, half.stop // CHUNK):
+                    cols = chunks[c]
                     nc.tensor.matmul_mx(
-                        out=y[m][:],
+                        out=y[c][:],
                         lhsT=w_codes[:, o * N : (o + 1) * N].bitcast(FP8X4),
                         lhsT_scale=w_scales[:, o * N : (o + 1) * N],
-                        rhs=xg[:, m * MW - h * H : (m + 1) * MW - h * H].bitcast(FP8X4),
-                        rhs_scale=xg_scales[4 * o :, m * MW : (m + 1) * MW],
+                        rhs=xg[o][h][:, cols.start - half.start : cols.stop - half.start].bitcast(FP8X4),
+                        rhs_scale=xg_scales[ROWS * o :, cols],
                         start=(o == 0),
                         stop=(o == PASSES - 1),
                     )
 
-        def y_cols(c):
-            m = c * CW // MW
-            return y[m][:, c * CW - m * MW : (c + 1) * CW - m * MW]
-
-        sq, t, a, e, r, q_t, g, th, res = [
-            pool.tile([P, S], F32, name=n) for n in ("sq", "t", "a", "e", "r", "q", "g", "th", "res")
+        ysq, base, inv_root, den, inv_den, quot, bounded, res = [
+            pool.tile([P, S], F32, name=name)
+            for name in ("ysq", "base", "inv_root", "den", "inv_den", "quot", "bounded", "res")
         ]
-        chunks = [slice(c * CW, (c + 1) * CW) for c in range(CH)]
         for c, cols in enumerate(chunks):
-            nc.scalar.activation(sq[:, cols], y_cols(c), ACT.Square, scale=0.5)
-        vsg0 = pool.tile([P, CW], F32, name="vsg0")
-        nc.vector.tensor_copy(vsg0[:], vs_sb[:].indirect(slot_sb[:, 0 : CW // 16]))
+            nc.scalar.activation(ysq[:, cols], y[c][:], ACT.Square, scale=0.5)
+        vsg_first = pool.tile([P, CHUNK], F32, name="vsg_first")
+        nc.vector.tensor_copy(vsg_first[:], vs_sb[:].indirect(entries(slot_sb, chunks[0])))
+        nc.vector.tensor_tensor(base[:, chunks[0]], vsg_first[:], ysq[:, chunks[0]], ALU.add)
+        for cols in chunks[1:]:
+            nc.vector.tensor_tensor(base[:, cols], vs_sb[:].indirect(entries(slot_sb, cols)), ysq[:, cols], ALU.add)
+        for cols in chunks:
+            nc.scalar.activation(inv_root[:, cols], base[:, cols], ACT.Abs_reciprocal_sqrt, scale=0.8, bias=TINY)
+        for cols in chunks:
+            nc.vector.scalar_tensor_tensor(den[:, cols], inv_root[:, cols], 5.0, base[:, cols], ALU.add, ALU.mult)
+        for cols in chunks:
+            nc.scalar.activation(inv_den[:, cols], den[:, cols], ACT.Abs_reciprocal_sqrt, scale=0.16, bias=0.01)
         for c, cols in enumerate(chunks):
-            looked_up = vsg0[:] if c == 0 else vs_sb[:].indirect(slot_sb[:, c * CW // 16 : (c + 1) * CW // 16])
-            nc.vector.tensor_tensor(t[:, cols], looked_up, sq[:, cols], ALU.add)
+            nc.vector.tensor_tensor(quot[:, cols], y[c][:], inv_den[:, cols], ALU.mult)
         for cols in chunks:
-            nc.scalar.activation(a[:, cols], t[:, cols], ACT.Abs_reciprocal_sqrt, scale=0.8, bias=1e-30)
-        for cols in chunks:
-            nc.vector.scalar_tensor_tensor(e[:, cols], a[:, cols], 5.0, t[:, cols], ALU.add, ALU.mult)
-        for cols in chunks:
-            nc.scalar.activation(r[:, cols], e[:, cols], ACT.Abs_reciprocal_sqrt, scale=0.16, bias=0.01)
-        for c, cols in enumerate(chunks):
-            nc.vector.tensor_tensor(q_t[:, cols], y_cols(c), r[:, cols], ALU.mult)
-        for cols in chunks:
-            nc.vector.scalar_tensor_tensor(upd[:, cols], wsg[:, cols], 0.1, q_t[:, cols], ALU.mult, ALU.add)
-        junk_u = pool.tile([P, S + 1], F32, name="junk_u")
-        quot = pool.tile([P, 1], F32, name="quot")
-        nc.vector.scalar_tensor_tensor(junk_u[:], upd[:], winv[:], upd[:], ALU.mult, ALU.mult, accum_out=quot[:])
+            nc.vector.scalar_tensor_tensor(upd[:, cols], wsg[:, cols], 0.1, quot[:, cols], ALU.mult, ALU.add)
+
+        scratch = pool.tile([P, S + 1], F32, name="scratch")
+        norm_sq = pool.tile([P, 1], F32, name="norm_sq")
+        nc.vector.scalar_tensor_tensor(scratch[:], upd[:], w_inv[:], upd[:], ALU.mult, ALU.mult, accum_out=norm_sq[:])
         ratio = pool.tile([P, 1], F32, name="ratio")
-        nc.gpsimd.tensor_tensor(ratio[:], quot[:], minus_half[:], ALU.pow)
-        rate08 = pool.tile([P, 1], F32, name="rate08")
-        nc.vector.tensor_scalar(rate08[:], rate_sb[:], 0.8, None, ALU.mult)
-        g = junk_u
-        fchunks = [slice(c * FW, (c + 1) * FW) for c in range(FCH)]
+        nc.gpsimd.tensor_tensor(ratio[:], norm_sq[:], minus_half[:], ALU.pow)
+
+        rate_scaled = pool.tile([P, 1], F32, name="rate_scaled")
+        nc.vector.tensor_scalar(rate_scaled[:], rate_sb[:], 0.8, None, ALU.mult)
         for cols in chunks:
-            nc.vector.scalar_tensor_tensor(g[:, cols], t[:, cols], rate08[:], a[:, cols], ALU.mult, ALU.mult)
-        for cols in fchunks:
-            nc.scalar.activation(th[:, cols], upd[:, cols], ACT.Tanh, scale=ratio[:])
-            nc.vector.tensor_tensor(res[:, cols], th[:, cols], g[:, cols], ALU.mult)
+            nc.vector.scalar_tensor_tensor(
+                scratch[:, cols], base[:, cols], rate_scaled[:], inv_root[:, cols], ALU.mult, ALU.mult
+            )
+        for cols in chunks:
+            nc.scalar.activation(bounded[:, cols], upd[:, cols], ACT.Tanh, scale=ratio[:])
+            nc.vector.tensor_tensor(res[:, cols], bounded[:, cols], scratch[:, cols], ALU.mult)
             nc.sync.dma_start(out[:, cols], res[:, cols])

from contextlib import ExitStack

import concourse.mybir as mybir

K, T, S, N, U = 1024, 2048, 512, 128, 1024
FLOPS = 2 * K * N * S

F32 = mybir.dt.float32
BF16 = mybir.dt.bfloat16
I32 = mybir.dt.int32
U32 = mybir.dt.uint32
U16 = mybir.dt.uint16
U8 = mybir.dt.uint8
FP8X4 = mybir.dt.float8_e4m3fn_x4
ACT = mybir.ActivationFunctionType
ALU = mybir.AluOpType

P = 128
PACK = 4
PASSES = K // (P * PACK)
QUADRANT = 32
ROWS = 4
BLOCK_PARTS = 8
LIST_COL = 16
HALF = S // 2
CHUNKS = 4
CHUNK = S // CHUNKS
NORM_EPS = 0.01 * S
TINY = 1e-30


def tile_picked_ylamb_bnd_p_kernel(
    tc, x_words, x_scales, w1, vs, ws, rate, offs, slot, out
):
    nc = tc.nc
    halves = [slice(h * HALF, (h + 1) * HALF) for h in range(2)]
    chunks = [slice(c * CHUNK, (c + 1) * CHUNK) for c in range(CHUNKS)]

    def entries(list_tile, cols):
        return list_tile[:, cols.start // LIST_COL : cols.stop // LIST_COL]

    with ExitStack() as ctx:
        pool = ctx.enter_context(tc.tile_pool(name="held", bufs=1))
        psum = ctx.enter_context(tc.psum_pool(name="psum", bufs=1))

        slot_sb = pool.tile([P, S // LIST_COL], U16, name="slot_sb")
        offs_sb = pool.tile([P, S // LIST_COL], U16, name="offs_sb")
        ws_sb = pool.tile([P, U], F32, name="ws_sb")
        w_raw = [pool.tile([P, PACK, N], F32, name="w_raw%d" % o) for o in range(PASSES)]
        x_sb = [pool.tile([P, T], I32, name="x_sb%d" % o) for o in range(PASSES)]
        xs_sb = pool.tile([P, T], U8, name="xs_sb")
        ones = pool.tile([P, 1], F32, name="ones")
        minus_half = pool.tile([P, 1], F32, name="minus_half")
        upd = pool.tile([P, S + 1], F32, name="upd")

        nc.vector.memset(xs_sb[:].bitcast(I32), 0)
        nc.vector.memset(ones[:], 1.0)
        nc.gpsimd.memset(minus_half[:], -0.5)
        nc.scalar.activation(upd[:, S : S + 1], ones[:], ACT.Abs_reciprocal_sqrt, scale=1.0 / NORM_EPS)

        def load_w(o):
            rows = w1[o * P * PACK : (o + 1) * P * PACK, :]
            nc.sync.dma_start(w_raw[o][:].rearrange("p j n -> p (j n)"), rows.rearrange("(p j) n -> p (j n)", j=PACK))

        nc.sync.dma_start(offs_sb[:], offs)
        nc.sync.dma_start(slot_sb[:], slot)
        load_w(0)
        for o in range(PASSES):
            nc.sync.dma_start(xs_sb[ROWS * o : P : BLOCK_PARTS, :].bitcast(I32), x_scales[o].bitcast(I32))
        nc.sync.dma_start(ws_sb[:], ws)
        load_w(1)
        for o in range(PASSES):
            nc.sync.dma_start(x_sb[o][:], x_words[o].rearrange("p c r -> p (c r)").bitcast(I32))

        xg_spread = pool.tile([P, S], U8, name="xg_spread", align_bytes=64)
        nc.vector.tensor_copy(xg_spread[:], xs_sb[:].indirect(offs_sb[:]))
        xg_scales = pool.tile([P, S], U8, name="xg_scales", align_bytes=64)
        nc.vector.tensor_copy(xg_scales[:].bitcast(I32), xg_spread[:].bitcast(I32))
        for o in range(PASSES):
            for i in range(1, ROWS):
                nc.sync.dma_start(
                    xg_scales[ROWS * o + i : P : QUADRANT, :].bitcast(I32),
                    xg_spread[ROWS * o + BLOCK_PARTS * i : P : QUADRANT, :].bitcast(I32),
                )

        wsg = pool.tile([P, S], F32, name="wsg")
        nc.vector.tensor_copy(wsg[:], ws_sb[:].indirect(slot_sb[:]))

        w_bf = pool.tile([P, PASSES, N, PACK], BF16, name="w_bf", tag="w_then_vs", align_bytes=64)
        for o in range(PASSES):
            nc.scalar.copy(w_bf[:, o], w_raw[o][:].rearrange("p j n -> p n j"))
        w_codes = pool.tile([P, PASSES * N], U32, name="w_codes", align_bytes=64)
        w_scales = pool.tile([P, PASSES * N], U8, name="w_scales", align_bytes=64)
        nc.vector.quantize_mx(
            out=w_codes[:].bitcast(FP8X4), scales=w_scales[:], in_=w_bf[:].rearrange("p o n j -> p (o n j)")
        )

        vs_sb = pool.tile([P, U], F32, name="vs_sb", tag="w_then_vs", align_bytes=64)
        nc.sync.dma_start(vs_sb[:], vs)

        wsq = pool.tile([P, S], F32, name="wsq")
        wsq_sum = pool.tile([P, 1], F32, name="wsq_sum")
        nc.scalar.activation(wsq[:], wsg[:], ACT.Square, accum_out=wsq_sum[:])

        def gather_words(o):
            tiles = [pool.tile([P, HALF], U32, name="xg%d_%d" % (o, h), align_bytes=64) for h in range(2)]
            for tile, cols in zip(tiles, halves):
                nc.vector.tensor_copy(tile[:], x_sb[o][:].bitcast(U32).indirect(entries(offs_sb, cols)))
            return tiles

        xg = [gather_words(0)]
        w_den = pool.tile([P, 1], F32, name="w_den", tag="w_den_then_rate")
        nc.vector.tensor_scalar(w_den[:], wsq_sum[:], NORM_EPS, None, ALU.add)
        w_inv = pool.tile([P, 1], F32, name="w_inv")
        nc.vector.reciprocal(w_inv[:], w_den[:])
        rate_sb = pool.tile([P, 1], F32, name="rate_sb", tag="w_den_then_rate")
        nc.sync.dma_start(rate_sb[:], rate)
        xg.append(gather_words(1))

        y = [psum.tile([P, CHUNK], F32, name="y%d" % c) for c in range(CHUNKS)]
        for h, half in enumerate(halves):
            for o in range(PASSES):
                for c in range(half.start // CHUNK, half.stop // CHUNK):
                    cols = chunks[c]
                    nc.tensor.matmul_mx(
                        out=y[c][:],
                        lhsT=w_codes[:, o * N : (o + 1) * N].bitcast(FP8X4),
                        lhsT_scale=w_scales[:, o * N : (o + 1) * N],
                        rhs=xg[o][h][:, cols.start - half.start : cols.stop - half.start].bitcast(FP8X4),
                        rhs_scale=xg_scales[ROWS * o :, cols],
                        start=(o == 0),
                        stop=(o == PASSES - 1),
                    )

        ysq, base, inv_root, den, inv_den, quot, bounded, res = [
            pool.tile([P, S], F32, name=name)
            for name in ("ysq", "base", "inv_root", "den", "inv_den", "quot", "bounded", "res")
        ]
        for c, cols in enumerate(chunks):
            nc.scalar.activation(ysq[:, cols], y[c][:], ACT.Square, scale=0.5)
        vsg_first = pool.tile([P, CHUNK], F32, name="vsg_first")
        nc.vector.tensor_copy(vsg_first[:], vs_sb[:].indirect(entries(slot_sb, chunks[0])))
        nc.vector.tensor_tensor(base[:, chunks[0]], vsg_first[:], ysq[:, chunks[0]], ALU.add)
        for cols in chunks[1:]:
            nc.vector.tensor_tensor(base[:, cols], vs_sb[:].indirect(entries(slot_sb, cols)), ysq[:, cols], ALU.add)
        for cols in chunks:
            nc.scalar.activation(inv_root[:, cols], base[:, cols], ACT.Abs_reciprocal_sqrt, scale=0.8, bias=TINY)
        for cols in chunks:
            nc.vector.scalar_tensor_tensor(den[:, cols], inv_root[:, cols], 5.0, base[:, cols], ALU.add, ALU.mult)
        for cols in chunks:
            nc.scalar.activation(inv_den[:, cols], den[:, cols], ACT.Abs_reciprocal_sqrt, scale=0.16, bias=0.01)
        for c, cols in enumerate(chunks):
            nc.vector.tensor_tensor(quot[:, cols], y[c][:], inv_den[:, cols], ALU.mult)
        for cols in chunks:
            nc.vector.scalar_tensor_tensor(upd[:, cols], wsg[:, cols], 0.1, quot[:, cols], ALU.mult, ALU.add)

        scratch = pool.tile([P, S + 1], F32, name="scratch")
        norm_sq = pool.tile([P, 1], F32, name="norm_sq")
        nc.vector.scalar_tensor_tensor(scratch[:], upd[:], w_inv[:], upd[:], ALU.mult, ALU.mult, accum_out=norm_sq[:])
        ratio = pool.tile([P, 1], F32, name="ratio")
        nc.gpsimd.tensor_tensor(ratio[:], norm_sq[:], minus_half[:], ALU.pow)

        rate_scaled = pool.tile([P, 1], F32, name="rate_scaled")
        nc.vector.tensor_scalar(rate_scaled[:], rate_sb[:], 0.8, None, ALU.mult)
        for cols in chunks:
            nc.vector.scalar_tensor_tensor(
                scratch[:, cols], base[:, cols], rate_scaled[:], inv_root[:, cols], ALU.mult, ALU.mult
            )
        for cols in chunks:
            nc.scalar.activation(bounded[:, cols], upd[:, cols], ACT.Tanh, scale=ratio[:])
            nc.vector.tensor_tensor(res[:, cols], bounded[:, cols], scratch[:, cols], ALU.mult)
            nc.sync.dma_start(out[:, cols], res[:, cols])
